import numpy as np, ml_dtypes
CORES = [8,136,40,168]
N = 4
import mx_ref
NC, ROOT = 128, 1
C = np.float32(0.029)
BF = ml_dtypes.bfloat16
def cut(t, i, w=512):
    return t[:, w * i:w * i + w]
def tile(rs):
    return np.stack(rs, axis=2).reshape(128, -1).astype(BF)
def pick(b):
    s = np.zeros((128, 128, 4), np.float32)
    s[np.arange(128), np.arange(128), b] = 1.0
    return mx_ref.quantize(s.reshape(128, 512).astype(BF))
def pk(c, s, i=0):
    return (np.ascontiguousarray(c[:, 512 * i:512 * i + 512]), mx_ref.live(s[:, 128 * i:128 * i + 128]))
def inputs(rng, e, E):
    def f(*shape):
        v = (rng.standard_normal(shape, dtype=np.float32) * np.exp2(rng.integers(-2, 3, shape[:-1] + (1,)))).astype(BF)
        return mx_ref.spread((v.astype(np.float32) * np.exp2(rng.integers(-E, E + 1, shape[:-2] + (1, 1))).astype(np.float32)).astype(BF), rng, e)
    def packed(k):
        c = np.zeros((N, 128, k * 512), np.uint8); s = np.zeros((N, 128, k * 128), np.uint8)
        for r in range(N):
            for i in range(k):
                a, b = mx_ref.quantize(f(128, 512)); c[r][:, 512 * i:512 * i + 512] = a; s[r][:, 128 * i:128 * i + 128] = mx_ref.plane(b, rng)
        return c, s
    d = {}
    d["wc"], d["ws"] = packed(1)
    d["a"] = f(N, 128, 512)
    d["bb"] = f(N, 128, 4 * 512)
    d["x"] = f(N, 128, 4 * NC)
    return d
def setup_inputs(rng):
    return inputs(rng, 0, 0)
def setup_inputs_blocks(rng):
    return inputs(rng, 2, 0)
def setup_inputs_wide(rng):
    return inputs(rng, 0, 3)
def reference(wc, ws, a, bb, x):
    S = [pick(t) for t in range(4)]; A = mx_ref.quantize(a[ROOT])
    V = [mx_ref.quantize(tile([mx_ref.matmul(S[t], pk(wc[j], ws[j])) + mx_ref.matmul(mx_ref.quantize(cut(bb[j], t)), A) * C for t in range(4)])) for j in range(N)]
    y = np.zeros((N, 128, N * NC), np.float32)
    for r in range(N):
        X = mx_ref.quantize(x[r])
        for j in range(N):
            y[r][:, NC * j:NC * j + NC] = mx_ref.matmul(V[j], X)
    return {"y": y}

import numpy as np
from concourse.bass import DstId, RemoteDMATransfer
from concourse.mybir import dt, AluOpType, ActivationFunctionType

NC = 128
W4 = 4 * NC
BANK = 512
SCALE = float(np.float32(0.029))

SCRATCH = {
    "a_t": ("sbuf", [128, W4], "bfloat16"),
    "bb_t": ("sbuf", [128, 4 * W4], "bfloat16"),
    "x_t": ("sbuf", [128, W4], "bfloat16"),
    "z_t": ("sbuf", [128, W4 + 8], "bfloat16"),
    "v_t": ("sbuf", [128, W4], "bfloat16"),
    "m_t": ("sbuf", [128, 4 * NC], "float32"),
    "y_t": ("sbuf", [128, 4 * NC], "float32"),
    "aq": ("sbuf", [128, NC], "float8_e4m3fn_x4"),
    "as_": ("sbuf", [128, NC], "uint8"),
    "bq": ("sbuf", [128, 4 * NC], "float8_e4m3fn_x4"),
    "bs": ("sbuf", [128, 4 * NC], "uint8"),
    "xq": ("sbuf", [128, NC], "float8_e4m3fn_x4"),
    "xs": ("sbuf", [128, NC], "uint8"),
    "pq": ("sbuf", [128, 4 * NC], "float8_e4m3fn_x4"),
    "ps": ("sbuf", [128, 4 * NC], "uint8"),
    "wq": ("sbuf", [128, NC], "float8_e4m3fn_x4"),
    "wsc": ("sbuf", [128, NC], "uint8"),
    "vq": ("sbuf", [128, 4 * NC], "float8_e4m3fn_x4"),
    "vs": ("sbuf", [128, 4 * NC], "uint8"),
    "d_p": ("psum", [128, 4 * BANK], "float32"),
    "m_p": ("psum", [128, 4 * BANK], "float32"),
}
SEMAPHORES = (["ld_a", "ld_b", "ld_w", "ld_x", "zero", "band", "q_a", "q_b", "q_x", "q_p", "q_v", "mm_d", "added",
               "out_a", "out_v", "in_a"]
              + ["mm%d" % b for b in range(4)] + ["sc%d" % b for b in range(4)] + ["in_v%d" % j for j in range(4)]
              + ["mmy%d" % j for j in range(4)] + ["cp%d" % j for j in range(4)] + ["st%d" % j for j in range(4)])


def rank_program(g, core, T, topo):
    rank = T.rank_of(core)
    if rank is None:
        return
    n, root = len(T.cores), T.root
    is_root = rank == root
    others = [(rank + k) % n for k in range(1, n)]

    def col(j, w=NC):
        return slice(w * j, w * j + w)

    def send(src, sem, local):
        mask = topo.mask(core, T.cores[others[0]])
        ids = []
        for o in others:
            mask &= topo.mask(core, T.cores[o])
            rid, pid = topo.addr(T.cores[o], core)
            ids.append(DstId(rid=rid, pnc=pid))
        g.remote_dma_fused([RemoteDMATransfer(dst_ids=ids, dma_engine_mask=mask, remote_sem=sem, srcs=[src],
                                              dsts=[src] * len(ids))], local_sem=local)
        return bin(mask).count("1")

    engines = bin(topo.mask(core, T.cores[others[0]])).count("1")

    q2 = g.sync if is_root else g.scalar
    if is_root:
        g.sync.dma_start(T.a_t[:], T.a[:]).then_inc(T.sem.ld_a, 16)
    g.sync.dma_start(T.bb_t[:], T.bb[:]).then_inc(T.sem.ld_b, 16)
    q2.dma_start(T.wq[:].bitcast(dt.uint8), T.wc[:]).then_inc(T.sem.ld_w, 16)
    q2.dma_start(T.wsc[:], T.ws[:]).then_inc(T.sem.ld_w, 16)
    q2.dma_start(T.x_t[:], T.x[:]).then_inc(T.sem.ld_x, 16)

    def band():
        g.wait_ge(T.sem.zero, 1)
        g.affine_select(T.z_t[:], T.z_t[:], [[1, W4 + 8]], AluOpType.not_equal, 1.0, -3, -4).then_inc(T.sem.band, 1)

    if is_root:
        g.wait_ge(T.sem.q_a, 1)
        send(T.aq[:].bitcast(dt.uint8), T.sem.in_a, T.sem.out_a)
        send(T.as_[:], T.sem.in_a, T.sem.out_a)
    band()
    g.wait_ge(T.sem.q_v, 1)
    send(T.vq[:, col(rank)].bitcast(dt.uint8), T.sem["in_v%d" % rank], T.sem.out_v)
    send(T.vs[:, col(rank)], T.sem["in_v%d" % rank], T.sem.out_v)
    if is_root:
        g.wait_ge(T.sem.out_a, 2 * engines)
    g.wait_ge(T.sem.out_v, 2 * engines)

    v = g.vector
    v.memset(T.z_t[:], 0.0).then_inc(T.sem.zero, 1)

    def q_bands():
        v.wait_ge(T.sem.band, 1)
        for b in range(4):
            v.quantize_mx(T.pq[:, col(b)], T.ps[:, col(b)], T.z_t[:, 3 - b:3 - b + W4]).then_inc(T.sem.q_p, 1)

    if is_root:
        v.wait_ge(T.sem.ld_a, 16)
        v.quantize_mx(T.aq[:], T.as_[:], T.a_t[:]).then_inc(T.sem.q_a, 1)
    else:
        q_bands()
    v.wait_ge(T.sem.ld_b, 16)
    for b in range(4):
        v.quantize_mx(T.bq[:, col(b)], T.bs[:, col(b)], T.bb_t[:, col(b, W4)]).then_inc(T.sem.q_b, 1)
    if is_root:
        q_bands()
    v.wait_ge(T.sem.ld_x, 16)
    v.quantize_mx(T.xq[:], T.xs[:], T.x_t[:]).then_inc(T.sem.q_x, 1)

    for b in range(4):
        g.scalar.wait_ge(T.sem["mm%d" % b], 1)
        g.scalar.activation(T.m_t[:, col(b)], T.m_p[:, BANK * b:BANK * b + NC], ActivationFunctionType.Copy,
                            scale=SCALE).then_inc(T.sem["sc%d" % b], 1)
    v.wait_ge(T.sem.mm_d, 4)
    for b in range(4):
        v.wait_ge(T.sem["sc%d" % b], 1)
        v.tensor_tensor(T.v_t[:, b:W4:4], T.d_p[:, BANK * b:BANK * b + NC], T.m_t[:, col(b)],
                        AluOpType.add).then_inc(T.sem.added, 1)
    v.wait_ge(T.sem.added, 4)
    v.quantize_mx(T.vq[:, col(rank)], T.vs[:, col(rank)], T.v_t[:]).then_inc(T.sem.q_v, 1)

    t = g.tensor
    t.wait_ge(T.sem.q_p, 4)
    t.wait_ge(T.sem.ld_w, 32)
    for b in range(4):
        t.matmul_mx(T.d_p[:, BANK * b:BANK * b + NC], T.pq[:, col(b)], T.ps[:, col(b)], T.wq[:], T.wsc[:],
                    True, True).then_inc(T.sem.mm_d, 1)
    t.wait_ge(T.sem.q_b, 4)
    if is_root:
        t.wait_ge(T.sem.q_a, 1)
    else:
        t.wait_ge(T.sem.in_a, 2 * engines)
    for b in range(4):
        t.matmul_mx(T.m_p[:, BANK * b:BANK * b + NC], T.bq[:, col(b)], T.bs[:, col(b)], T.aq[:], T.as_[:],
                    True, True).then_inc(T.sem["mm%d" % b], 1)

    order = [rank] + ([] if is_root else [root]) + [j for j in others[::-1] if j != root]
    t.wait_ge(T.sem.q_x, 1)
    for i, j in enumerate(order):
        if j == rank:
            t.wait_ge(T.sem.q_v, 1)
        else:
            t.wait_ge(T.sem["in_v%d" % j], 2 * engines)
        t.matmul_mx(T.m_p[:, BANK * i:BANK * i + NC], T.vq[:, col(j)], T.vs[:, col(j)], T.xq[:], T.xs[:],
                    True, True).then_inc(T.sem["mmy%d" % i], 1)
        src, dst = T.m_p[:, BANK * i:BANK * i + NC], T.y_t[:, col(i)]
        if i % 2 == 0:
            v.wait_ge(T.sem["mmy%d" % i], 1)
            v.tensor_copy(dst, src).then_inc(T.sem["cp%d" % i], 1)
            q = g.sync
        else:
            g.scalar.wait_ge(T.sem["mmy%d" % i], 1)
            g.scalar.activation(dst, src, ActivationFunctionType.Copy).then_inc(T.sem["cp%d" % i], 1)
            q = g.scalar
        q.wait_ge(T.sem["cp%d" % i], 1)
        q.dma_start(T.y[:, col(j)], dst).then_inc(T.sem["st%d" % i], 16)
    for i in range(n):
        (g.sync if i % 2 == 0 else g.scalar).wait_ge(T.sem["st%d" % i], 16)
